import numpy as np
import ml_dtypes


def mxq(x, axis, fmt="e4m3"):
    dtype, down = {"e4m3": (ml_dtypes.float8_e4m3fn, 7), "e5m2": (ml_dtypes.float8_e5m2, 14)}[fmt]
    v = np.moveaxis(np.asarray(x, np.float32).astype(ml_dtypes.bfloat16).astype(np.float64), axis, -1)
    blocks = v.reshape(v.shape[:-1] + (-1, 32))
    amax = np.abs(blocks).max(-1, keepdims=True)
    byte = np.maximum(np.where(amax > 0, np.frexp(amax)[1] - 1 + 127, 0) - down, 1)
    scale = np.exp2(byte - 127.0)
    codes = (blocks / scale).astype(np.float32).astype(dtype).astype(np.float64)
    return np.moveaxis((codes * scale).reshape(v.shape), -1, axis)


WIDE = False


def mx_kscale(k):
    if not WIDE:
        return np.ones(k)
    levels = np.array([10, -10, 5, -5, 0])
    if k % 512:
        return np.exp2(np.random.permutation(np.resize(levels, k // 32))).repeat(32)
    a = np.empty((k // 512, 16))
    for p in range(k // 512):
        a[p, :8] = np.random.permutation(np.resize(levels, 8))
        for g in range(8):
            far = levels[np.abs(levels - a[p, g]) >= 10]
            a[p, g + 8] = far[np.random.randint(len(far))]
    return np.exp2(a.ravel()).repeat(32)


def f64(x):
    return np.asarray(x).astype(np.float64)


def striped(idx):
    return np.tile(idx.reshape(-1, 16).T, (8, 1)).astype(np.uint16)


def unstriped(offs):
    return offs[:16].T.reshape(-1).astype(np.int64)


def pack_weight(w):
    k, n = w.shape
    w = f64(np.asarray(w, np.float32).astype(ml_dtypes.bfloat16)).reshape(k // 32, 32, n)
    amax = np.abs(w).max(1)
    byte = np.clip(np.where(amax > 0, np.frexp(amax)[1] - 1 + 127 - 7, 1), 1, 254)
    scaled = (w * np.exp2(127.0 - byte)[:, None, :]).reshape(k, n).astype(np.float32)
    words = np.ascontiguousarray(scaled.reshape(k // 512, 128, 4, n).transpose(0, 1, 3, 2)).astype(ml_dtypes.float8_e4m3fn).view(np.uint8)
    return words, np.ascontiguousarray(byte.astype(np.uint8).reshape(k // 512, 16, n))


def unpack_weight(words, scales):
    g, p, n, _ = words.shape
    vals = np.ascontiguousarray(words).view(ml_dtypes.float8_e4m3fn).astype(np.float64) * np.repeat(np.exp2(scales.astype(np.float64) - 127.0), 8, axis=1)[..., None]
    return vals.transpose(0, 1, 3, 2).reshape(g * 512, n)


K, T, S, V = 512, 1024, 512, 512
P = 2 ** 7


def setup_inputs():
    n = np.random.standard_normal
    s = mx_kscale(K)[:, None]
    packed_xT = pack_weight(n((K, T)) * s)
    packed_eT = pack_weight(n((K, T)) * s)
    return {
        "x_words": packed_xT[0],
        "x_scales": packed_xT[1],
        "hT": (n((K, V)) / np.sqrt(K) / s).astype(np.float32),
        "e_words": packed_eT[0],
        "e_scales": packed_eT[1],
        "lena": (np.tile(np.random.uniform(0.4, 2.0, T), (P, 1))).astype(np.float32),
        "lenb": (np.tile(np.random.uniform(0.4, 2.0, T), (P, 1))).astype(np.float32),
        "idf": (np.random.uniform(0.5, 4.0, (V, 1))).astype(np.float32),
        "offs": striped(np.random.permutation(T)[:S]),
    }


def reference(x_words, x_scales, hT, e_words, e_scales, lena, lenb, idf, offs):
    hTq = mxq(f64(hT), 0, "e4m3")
    xq = unpack_weight(x_words, x_scales)[:, unstriped(offs)]
    ya = hTq.T @ xq
    tfa = np.log(np.exp(ya) + 1.0)
    e_offs = unpack_weight(e_words, e_scales)[:, unstriped(offs)]
    yb = hTq.T @ e_offs
    tfb = np.log(np.exp(yb) + 1.0)
    tf = 2.2 * (tfa / (0.6 * (f64(lena)[:1][:, unstriped(offs)]) + 0.4)) + tfb / (0.75 * (f64(lenb)[:1][:, unstriped(offs)]) + 0.25)
    return f64(idf) * (tf / (tf + 1.2))

@@ -1,0 +1,214 @@
+from contextlib import ExitStack
+
+import concourse.mybir as mybir
+from concourse.masks import make_identity
+
+K, T, S, V = 512, 1024, 512, 512
+FLOPS = 2 * 2 * K * S * V
+BYTES = 2 * (K * T + 16 * T) + 4 * K * V + 2 * 4 * T + 4 * V + 2 * 128 * (S // 16) + 4 * V * S
+
+F32 = mybir.dt.float32
+BF16 = mybir.dt.bfloat16
+I32 = mybir.dt.int32
+U32 = mybir.dt.uint32
+U16 = mybir.dt.uint16
+U8 = mybir.dt.uint8
+FP8X4 = mybir.dt.float8_e4m3fn_x4
+ALU = mybir.AluOpType
+ACT = mybir.ActivationFunctionType
+
+P = 128
+HALF = 256
+LOG_FLOOR = 2.0 ** -50
+
+
+def tile_picked_ybm25f_sat_p_kernel(
+    tc, x_words, x_scales, hT, e_words, e_scales, lena, lenb, idf, offs, out
+):
+    nc = tc.nc
+    with ExitStack() as ctx:
+        keep = ctx.enter_context(tc.tile_pool(name="keep", bufs=1))
+        psum = ctx.enter_context(tc.psum_pool(name="psum", bufs=1))
+
+        offsets = keep.tile([P, S // 16], U16, name="offsets")
+        word_tab = [keep.tile([P, T], U32, name="word_tab%d" % f, tag="tab%d" % f, align_bytes=64) for f in range(2)]
+        scale_tab = [keep.tile([P, T], U8, name="scale_tab%d" % f, align_bytes=64) for f in range(2)]
+        len_tab = [keep.tile([P, T], F32, name="len_tab%d" % f, align_bytes=64) for f in range(2)]
+        h_raw = [keep.tile([P, 4, HALF], F32, name="h_raw%d" % h, align_bytes=64) for h in range(2)]
+        idf_col = keep.tile([P, 4], F32, name="idf_col")
+        ident = keep.tile([P, P], F32, name="ident", align_bytes=64)
+
+        for f in range(2):
+            nc.vector.memset(len_tab[f][0:96, :], 0.0)
+
+        def load_scales(queue, f, scales, quadrants):
+            for q in quadrants:
+                queue.dma_start(
+                    out=scale_tab[f][32 * q : 32 * q + 32, :].bitcast(I32),
+                    in_=scales[0, 4 * q : 4 * q + 4, :].bitcast(I32).partition_broadcast(8),
+                )
+
+        def load_words(f, words):
+            nc.sync.dma_start(
+                out=word_tab[f][:].bitcast(I32),
+                in_=words[0].rearrange("p n r -> p (n r)").bitcast(I32),
+            )
+
+        def load_terms(h):
+            nc.sync.dma_start(
+                out=h_raw[h][:],
+                in_=hT[:, h * HALF : (h + 1) * HALF].rearrange("(p r) t -> p r t", r=4),
+            )
+
+        nc.sync.dma_start(offsets[:], offs)
+        load_scales(nc.sync, 0, x_scales, range(4))
+        load_terms(0)
+        nc.sync.dma_start(out=len_tab[0][96:P, :], in_=lena[0:32, :])
+        nc.sync.dma_start(out=len_tab[1][96:P, :], in_=lenb[0:32, :])
+        load_words(0, x_words)
+        load_terms(1)
+        load_scales(nc.sync, 1, e_scales, range(4))
+        load_words(1, e_words)
+        make_identity(nc, ident[:])
+        with nc.allow_non_contiguous_dma(reason="one value a partition"):
+            nc.gpsimd.dma_start(out=idf_col[:], in_=idf.rearrange("(b p) o -> p (b o)", p=P))
+
+        h_codes = [keep.tile([P, HALF], U32, name="h_codes%d" % h, align_bytes=64) for h in range(2)]
+        h_scales = [keep.tile([P, HALF], U8, name="h_scales%d" % h, align_bytes=64) for h in range(2)]
+        h_bf = [keep.tile([P, HALF, 4], BF16, name="h_bf%d" % h, align_bytes=64) for h in range(2)]
+        words = [keep.tile([P, S], U32, name="words%d" % f, align_bytes=64) for f in range(2)]
+        scales = [keep.tile([P, S], U8, name="scales%d" % f, align_bytes=64) for f in range(2)]
+
+        def cast_terms(h):
+            nc.vector.tensor_copy(
+                out=h_bf[h][:],
+                in_=h_raw[h][:].rearrange("p r t -> p t r"),
+            )
+
+        def quantize_terms(h):
+            nc.vector.quantize_mx(
+                out=h_codes[h][:].bitcast(FP8X4),
+                scales=h_scales[h][:],
+                in_=h_bf[h][:].rearrange("p t r -> p (t r)"),
+            )
+
+        def gather(dst, table, d):
+            picked = offsets[:, d * HALF // 16 : (d + 1) * HALF // 16]
+            nc.vector.tensor_copy(dst[:, d * HALF : (d + 1) * HALF], table[:].indirect(picked))
+
+        factor = keep.tile([P, 2, 2, 4], F32, name="factor")
+        norm = keep.tile([P, 2, 2, 4], F32, name="norm")
+
+        picked_lens = [keep.tile([P, S], F32, name="picked_len%d" % f, align_bytes=64) for f in range(2)]
+        for f in range(2):
+            nc.scalar.activation(picked_lens[f][:], len_tab[f][:].indirect(offsets[:]), ACT.Copy)
+
+        def length_norm(f, slope, base, bank):
+            picked_len = picked_lens[f]
+            turned = psum.tile([P, 4, P], F32, name="turned%d" % f, tag="bank%d" % bank)
+            for b in range(4):
+                nc.tensor.transpose(turned[:, b, :], picked_len[:, b * P : (b + 1) * P], ident[:])
+            for s, sign in enumerate((1.0, -1.0)):
+                nc.vector.tensor_scalar(
+                    norm[:, f, s, :], turned[:, :, P - 1], sign * slope, sign * base, ALU.mult, ALU.add
+                )
+            nc.vector.reciprocal(factor[:, f].rearrange("p s b -> p (s b)"), norm[:, f].rearrange("p s b -> p (s b)"))
+
+        units = [(h, d) for h in range(2) for d in range(2)]
+        score = {}
+        sig = [keep.tile([P, 2, 2 * HALF], F32, name="sig%d" % u) for u in range(4)]
+
+        def product(f, u):
+            h, d = units[u]
+            bank = psum.tile([P, 2, HALF], F32, name="score%d%d" % (f, u), tag="bank%d" % (4 * f + u))
+            for i in range(2):
+                docs = slice((2 * d + i) * P, (2 * d + i + 1) * P)
+                nc.tensor.matmul_mx(
+                    out=bank[:, i, :],
+                    lhsT=words[f][:, docs].bitcast(FP8X4),
+                    lhsT_scale=scales[f][:, docs],
+                    rhs=h_codes[h][:].bitcast(FP8X4),
+                    rhs_scale=h_scales[h][:],
+                    start=True,
+                    stop=True,
+                )
+            score[f, u] = bank
+            nc.scalar.activation(sig[u][:, f, :], bank[:].rearrange("p i t -> p (i t)"), ACT.Sigmoid, scale=-1.0)
+
+        gather(scales[0], scale_tab[0], 0)
+        gather(scales[0], scale_tab[0], 1)
+        cast_terms(0)
+        gather(words[0], word_tab[0], 0)
+        quantize_terms(0)
+        gather(words[0], word_tab[0], 1)
+        product(0, 0)
+        product(0, 1)
+        cast_terms(1)
+        quantize_terms(1)
+        product(0, 2)
+        product(0, 3)
+        length_norm(0, 0.6 / 2.2, 0.4 / 2.2, 7)
+        gather(scales[1], scale_tab[1], 0)
+        gather(words[1], word_tab[1], 0)
+        gather(scales[1], scale_tab[1], 1)
+        gather(words[1], word_tab[1], 1)
+        for u in (0, 2, 1, 3):
+            product(1, u)
+
+        neg_idf = keep.tile([P, 4], F32, name="neg_idf")
+        nc.gpsimd.tensor_scalar(neg_idf[:], idf_col[:], -1.2, 0.0, ALU.mult, ALU.add)
+
+        lin = keep.tile([P, 2, 4, 2, HALF], F32, name="lin", tag="tab1", align_bytes=64)
+        for f in range(2):
+            for u in range(4):
+                h, d = units[u]
+                for i in range(2):
+                    b = 2 * d + i
+                    nc.vector.tensor_scalar(
+                        lin[:, f, u, i, :], score[f, u][:, i, :], factor[:, f, 0, b : b + 1], None, ALU.mult
+                    )
+                if (f, u) == (0, 0):
+                    length_norm(1, 0.75, 0.25, 0)
+
+        total = [psum.tile([P, S], F32, name="total%d" % tb, tag="bank%d" % tb) for tb in range(4)]
+        for u in range(4):
+            h, d = units[u]
+            logs = keep.tile([P, 2, 2 * HALF], F32, name="logs%d" % u)
+            nc.scalar.activation(
+                logs[:].rearrange("p f t -> p (f t)"), sig[u][:].rearrange("p f t -> p (f t)"), ACT.Ln, bias=LOG_FLOOR
+            )
+            part = keep.tile([P, 2, 2, HALF], F32, name="part%d" % u, align_bytes=64)
+            for i in range(2):
+                b = 2 * d + i
+                for f in range(2):
+                    nc.vector.scalar_tensor_tensor(
+                        part[:, f, i, :], logs[:, f, i * HALF : (i + 1) * HALF], factor[:, f, 1, b : b + 1],
+                        lin[:, f, u, i, :], ALU.mult, ALU.max,
+                    )
+            for i in range(2):
+                b = 2 * d + i
+                for e in range(2):
+                    for f in range(2):
+                        nc.tensor.matmul(
+                            total[2 * h + e][:, b * P : (b + 1) * P],
+                            part[:, f, i, e * P : (e + 1) * P],
+                            ident[:],
+                            start=(f == 0),
+                            stop=(f == 1),
+                            is_transpose=True,
+                        )
+
+        for tb in range(4):
+            root = keep.tile([P, S], F32, name="root%d" % tb)
+            nc.scalar.activation(root[:], total[tb][:], ACT.Abs_reciprocal_sqrt, bias=1.2)
+            drop = keep.tile([P, S], F32, name="drop%d" % tb)
+            result = keep.tile([P, S], F32, name="result%d" % tb)
+            if tb < 3:
+                nc.vector.scalar_tensor_tensor(drop[:], root[:], neg_idf[:, tb : tb + 1], root[:], ALU.mult, ALU.mult)
+                nc.vector.tensor_scalar(result[:], drop[:], idf_col[:, tb : tb + 1], None, ALU.add)
+            else:
+                nc.scalar.activation(drop[:], root[:], ACT.Square)
+                nc.vector.tensor_scalar(
+                    result[:], drop[:], neg_idf[:, tb : tb + 1], idf_col[:, tb : tb + 1], ALU.mult, ALU.add
+                )
+            nc.sync.dma_start(out=out[tb * P : (tb + 1) * P, :], in_=result[:])

@@ -99,6 +99,9 @@ def tile_picked_ybm25f_sat_p_kernel(
         factor = keep.tile([P, 2, 2, 4], F32, name="factor")
         norm = keep.tile([P, 2, 2, 4], F32, name="norm")
 
+        warm = keep.tile([P, 2], F32, name="warm")
+        nc.vector.memset(warm[:, 0:1], 0.0)
+        nc.scalar.activation(warm[:, 1:2], warm[:, 0:1], ACT.Sigmoid)
         picked_lens = [keep.tile([P, S], F32, name="picked_len%d" % f, align_bytes=64) for f in range(2)]
         for f in range(2):
             nc.scalar.activation(picked_lens[f][:], len_tab[f][:].indirect(offsets[:]), ACT.Copy)

@@ -32,14 +32,13 @@ def tile_picked_ybm25f_sat_p_kernel(
 
         offsets = keep.tile([P, S // 16], U16, name="offsets")
         word_tab = [keep.tile([P, T], U32, name="word_tab%d" % f, tag="tab%d" % f, align_bytes=64) for f in range(2)]
-        scale_tab = [keep.tile([P, T], U8, name="scale_tab%d" % f, align_bytes=64) for f in range(2)]
-        len_tab = [keep.tile([P, T], F32, name="len_tab%d" % f, align_bytes=64) for f in range(2)]
-        h_raw = [keep.tile([P, 4, HALF], F32, name="h_raw%d" % h, align_bytes=64) for h in range(2)]
+        scale_tab = [keep.tile([P, T], U8, name="scale_tab%d" % f, tag="stab%d" % f, align_bytes=64) for f in range(2)]
+        len_tab = keep.tile([P, T], F32, name="len_tab", align_bytes=64)
+        h_raw = [keep.tile([P, 4, HALF], F32, name="h_raw%d" % h, tag="raw%d" % h, align_bytes=64) for h in range(2)]
         idf_col = keep.tile([P, 4], F32, name="idf_col")
         ident = keep.tile([P, P], F32, name="ident", align_bytes=64)
 
-        for f in range(2):
-            nc.vector.memset(len_tab[f][0:96, :], 0.0)
+        nc.vector.memset(len_tab[0:96, :], 0.0)
 
         def load_scales(queue, f, scales, quadrants):
             for q in quadrants:
@@ -63,130 +62,136 @@ def tile_picked_ybm25f_sat_p_kernel(
         nc.sync.dma_start(offsets[:], offs)
         load_scales(nc.sync, 0, x_scales, range(4))
         load_terms(0)
-        nc.sync.dma_start(out=len_tab[0][96:P, :], in_=lena[0:32, :])
-        nc.sync.dma_start(out=len_tab[1][96:P, :], in_=lenb[0:32, :])
+        nc.sync.dma_start(out=len_tab[96:112, :], in_=lena[0:16, :])
+        nc.sync.dma_start(out=len_tab[112:128, :], in_=lenb[0:16, :])
         load_words(0, x_words)
         load_terms(1)
         load_scales(nc.sync, 1, e_scales, range(4))
         load_words(1, e_words)
-        make_identity(nc, ident[:])
         with nc.allow_non_contiguous_dma(reason="one value a partition"):
-            nc.gpsimd.dma_start(out=idf_col[:], in_=idf.rearrange("(b p) o -> p (b o)", p=P))
+            nc.sync.dma_start(out=idf_col[:], in_=idf.rearrange("(b p) o -> p (b o)", p=P))
+        make_identity(nc, ident[:])
 
-        h_codes = [keep.tile([P, HALF], U32, name="h_codes%d" % h, align_bytes=64) for h in range(2)]
-        h_scales = [keep.tile([P, HALF], U8, name="h_scales%d" % h, align_bytes=64) for h in range(2)]
+        h_codes = keep.tile([P, V], U32, name="h_codes", align_bytes=64)
+        h_scales = keep.tile([P, V], U8, name="h_scales", align_bytes=64)
         h_bf = [keep.tile([P, HALF, 4], BF16, name="h_bf%d" % h, align_bytes=64) for h in range(2)]
         words = [keep.tile([P, S], U32, name="words%d" % f, align_bytes=64) for f in range(2)]
         scales = [keep.tile([P, S], U8, name="scales%d" % f, align_bytes=64) for f in range(2)]
 
-        def cast_terms(h):
-            nc.vector.tensor_copy(
-                out=h_bf[h][:],
-                in_=h_raw[h][:].rearrange("p r t -> p t r"),
+        def cast_terms(h, copy, cols):
+            copy(
+                out=h_bf[h][:, cols, :].rearrange("p (c i) r -> p c r i", i=4),
+                in_=h_raw[h][:, :, cols].rearrange("p r (c i) -> p c r i", i=4),
             )
 
         def quantize_terms(h):
             nc.vector.quantize_mx(
-                out=h_codes[h][:].bitcast(FP8X4),
-                scales=h_scales[h][:],
+                out=h_codes[:, h * HALF : (h + 1) * HALF].bitcast(FP8X4),
+                scales=h_scales[:, h * HALF : (h + 1) * HALF],
                 in_=h_bf[h][:].rearrange("p t r -> p (t r)"),
             )
 
-        def gather(dst, table, d):
-            picked = offsets[:, d * HALF // 16 : (d + 1) * HALF // 16]
-            nc.vector.tensor_copy(dst[:, d * HALF : (d + 1) * HALF], table[:].indirect(picked))
+        def gather(dst, table, first, count):
+            picked = offsets[:, first // 16 : (first + count) // 16]
+            nc.vector.tensor_copy(dst[:, first : first + count], table[:].indirect(picked))
 
-        factor = keep.tile([P, 2, 2, 4], F32, name="factor")
+        factor = keep.tile([P, 2, 2, 4], F32, name="factor", tag="stab1", align_bytes=64)
         norm = keep.tile([P, 2, 2, 4], F32, name="norm")
 
         warm = keep.tile([P, 2], F32, name="warm")
         nc.vector.memset(warm[:, 0:1], 0.0)
         nc.scalar.activation(warm[:, 1:2], warm[:, 0:1], ACT.Sigmoid)
-        picked_lens = [keep.tile([P, S], F32, name="picked_len%d" % f, align_bytes=64) for f in range(2)]
-        for f in range(2):
-            nc.scalar.activation(picked_lens[f][:], len_tab[f][:].indirect(offsets[:]), ACT.Copy)
-
-        def length_norm(f, slope, base, bank):
-            picked_len = picked_lens[f]
-            turned = psum.tile([P, 4, P], F32, name="turned%d" % f, tag="bank%d" % bank)
+        def length_factors():
+            turned = psum.tile([P, 4, P], F32, name="turned", tag="bank7")
             for b in range(4):
                 nc.tensor.transpose(turned[:, b, :], picked_len[:, b * P : (b + 1) * P], ident[:])
-            for s, sign in enumerate((1.0, -1.0)):
-                nc.vector.tensor_scalar(
-                    norm[:, f, s, :], turned[:, :, P - 1], sign * slope, sign * base, ALU.mult, ALU.add
-                )
-            nc.vector.reciprocal(factor[:, f].rearrange("p s b -> p (s b)"), norm[:, f].rearrange("p s b -> p (s b)"))
+            for f, (slope, base) in enumerate(((0.6 / 2.2, 0.4 / 2.2), (0.75, 0.25))):
+                for s, sign in enumerate((1.0, -1.0)):
+                    nc.scalar.activation(
+                        norm[:, f, s, :], turned[:, :, 96 + 16 * f], ACT.Identity, bias=sign * base, scale=sign * slope
+                    )
 
         units = [(h, d) for h in range(2) for d in range(2)]
-        score = {}
-        sig = [keep.tile([P, 2, 2 * HALF], F32, name="sig%d" % u) for u in range(4)]
+        sig = keep.tile([P, 2, 4, V], F32, name="sig")
 
-        def product(f, u):
+        def product(f, dst, b, terms):
+            docs = slice(b * P, (b + 1) * P)
+            nc.tensor.matmul_mx(
+                out=dst,
+                lhsT=words[f][:, docs].bitcast(FP8X4),
+                lhsT_scale=scales[f][:, docs],
+                rhs=h_codes[:, terms].bitcast(FP8X4),
+                rhs_scale=h_scales[:, terms],
+                start=True,
+                stop=True,
+            )
+
+        title_score, body_score = [], []
+
+        def title_unit(u):
             h, d = units[u]
-            bank = psum.tile([P, 2, HALF], F32, name="score%d%d" % (f, u), tag="bank%d" % (4 * f + u))
+            terms = slice(h * HALF, (h + 1) * HALF)
+            bank = psum.tile([P, 2, HALF], F32, name="title_score%d" % u, tag="bank%d" % u)
             for i in range(2):
-                docs = slice((2 * d + i) * P, (2 * d + i + 1) * P)
-                nc.tensor.matmul_mx(
-                    out=bank[:, i, :],
-                    lhsT=words[f][:, docs].bitcast(FP8X4),
-                    lhsT_scale=scales[f][:, docs],
-                    rhs=h_codes[h][:].bitcast(FP8X4),
-                    rhs_scale=h_scales[h][:],
-                    start=True,
-                    stop=True,
-                )
-            score[f, u] = bank
-            nc.scalar.activation(sig[u][:, f, :], bank[:].rearrange("p i t -> p (i t)"), ACT.Sigmoid, scale=-1.0)
+                product(0, bank[:, i, :], 2 * d + i, terms)
+            title_score.append(bank)
+            nc.scalar.activation(sig[:, 0, 2 * d : 2 * d + 2, terms], bank[:], ACT.Sigmoid, scale=-1.0)
 
-        gather(scales[0], scale_tab[0], 0)
-        gather(scales[0], scale_tab[0], 1)
-        cast_terms(0)
-        gather(words[0], word_tab[0], 0)
+        def body_unit(b):
+            bank = psum.tile([P, V], F32, name="body_score%d" % b, tag="bank%d" % (4 + b))
+            product(1, bank[:], b, slice(0, V))
+            body_score.append(bank)
+            nc.scalar.activation(sig[:, 1, b, :], bank[:], ACT.Sigmoid, scale=-1.0)
+
+        gather(scales[0], scale_tab[0], 0, HALF)
+        gather(scales[0], scale_tab[0], HALF, HALF)
+        cast_terms(0, nc.scalar.copy, slice(0, P))
+        cast_terms(0, nc.vector.tensor_copy, slice(P, HALF))
+        picked_len = keep.tile([P, S], F32, name="picked_len", tag="raw0", align_bytes=64)
+        nc.scalar.activation(picked_len[:], len_tab[:].indirect(offsets[:]), ACT.Copy)
         quantize_terms(0)
-        gather(words[0], word_tab[0], 1)
-        product(0, 0)
-        product(0, 1)
-        cast_terms(1)
+        gather(words[0], word_tab[0], 0, HALF)
+        title_unit(0)
+        gather(words[0], word_tab[0], HALF, HALF)
+        title_unit(1)
+        cast_terms(1, nc.vector.tensor_copy, slice(0, HALF))
         quantize_terms(1)
-        product(0, 2)
-        product(0, 3)
-        length_norm(0, 0.6 / 2.2, 0.4 / 2.2, 7)
-        gather(scales[1], scale_tab[1], 0)
-        gather(words[1], word_tab[1], 0)
-        gather(scales[1], scale_tab[1], 1)
-        gather(words[1], word_tab[1], 1)
-        for u in (0, 2, 1, 3):
-            product(1, u)
+        title_unit(2)
+        title_unit(3)
+        length_factors()
+        for d in range(2):
+            gather(scales[1], scale_tab[1], d * HALF, HALF)
+            for b in (2 * d, 2 * d + 1):
+                gather(words[1], word_tab[1], b * P, P)
+                body_unit(b)
+        nc.vector.reciprocal(factor[:].rearrange("p f s b -> p (f s b)"), norm[:].rearrange("p f s b -> p (f s b)"))
 
         neg_idf = keep.tile([P, 4], F32, name="neg_idf")
         nc.gpsimd.tensor_scalar(neg_idf[:], idf_col[:], -1.2, 0.0, ALU.mult, ALU.add)
 
-        lin = keep.tile([P, 2, 4, 2, HALF], F32, name="lin", tag="tab1", align_bytes=64)
-        for f in range(2):
-            for u in range(4):
-                h, d = units[u]
-                for i in range(2):
-                    b = 2 * d + i
-                    nc.vector.tensor_scalar(
-                        lin[:, f, u, i, :], score[f, u][:, i, :], factor[:, f, 0, b : b + 1], None, ALU.mult
-                    )
-                if (f, u) == (0, 0):
-                    length_norm(1, 0.75, 0.25, 0)
+        lin = keep.tile([P, 2, 4, V], F32, name="lin", tag="tab1", align_bytes=64)
+        for u, (h, d) in enumerate(units):
+            for i in range(2):
+                b = 2 * d + i
+                nc.vector.tensor_scalar(
+                    lin[:, 0, b, h * HALF : (h + 1) * HALF], title_score[u][:, i, :], factor[:, 0, 0, b : b + 1], None, ALU.mult
+                )
+        for b in range(4):
+            nc.vector.tensor_scalar(lin[:, 1, b, :], body_score[b][:], factor[:, 1, 0, b : b + 1], None, ALU.mult)
 
         total = [psum.tile([P, S], F32, name="total%d" % tb, tag="bank%d" % tb) for tb in range(4)]
         for u in range(4):
             h, d = units[u]
-            logs = keep.tile([P, 2, 2 * HALF], F32, name="logs%d" % u)
-            nc.scalar.activation(
-                logs[:].rearrange("p f t -> p (f t)"), sig[u][:].rearrange("p f t -> p (f t)"), ACT.Ln, bias=LOG_FLOOR
-            )
+            terms = slice(h * HALF, (h + 1) * HALF)
+            logs = keep.tile([P, 2, 2, HALF], F32, name="logs%d" % u)
+            nc.scalar.activation(logs[:], sig[:, :, 2 * d : 2 * d + 2, terms], ACT.Ln, bias=LOG_FLOOR)
             part = keep.tile([P, 2, 2, HALF], F32, name="part%d" % u, align_bytes=64)
             for i in range(2):
                 b = 2 * d + i
                 for f in range(2):
                     nc.vector.scalar_tensor_tensor(
-                        part[:, f, i, :], logs[:, f, i * HALF : (i + 1) * HALF], factor[:, f, 1, b : b + 1],
-                        lin[:, f, u, i, :], ALU.mult, ALU.max,
+                        part[:, f, i, :], logs[:, f, i, :], factor[:, f, 1, b : b + 1],
+                        lin[:, f, b, terms], ALU.mult, ALU.max,
                     )
             for i in range(2):
                 b = 2 * d + i
@@ -203,15 +208,18 @@ def tile_picked_ybm25f_sat_p_kernel(
 
         for tb in range(4):
             root = keep.tile([P, S], F32, name="root%d" % tb)
-            nc.scalar.activation(root[:], total[tb][:], ACT.Abs_reciprocal_sqrt, bias=1.2)
             drop = keep.tile([P, S], F32, name="drop%d" % tb)
             result = keep.tile([P, S], F32, name="result%d" % tb)
+            rows = slice(tb * P, (tb + 1) * P)
+            nc.scalar.activation(root[:], total[tb][:], ACT.Abs_reciprocal_sqrt, bias=1.2)
             if tb < 3:
                 nc.vector.scalar_tensor_tensor(drop[:], root[:], neg_idf[:, tb : tb + 1], root[:], ALU.mult, ALU.mult)
                 nc.vector.tensor_scalar(result[:], drop[:], idf_col[:, tb : tb + 1], None, ALU.add)
+                nc.sync.dma_start(out=out[rows, :], in_=result[:])
             else:
-                nc.scalar.activation(drop[:], root[:], ACT.Square)
-                nc.vector.tensor_scalar(
-                    result[:], drop[:], neg_idf[:, tb : tb + 1], idf_col[:, tb : tb + 1], ALU.mult, ALU.add
-                )
-            nc.sync.dma_start(out=out[tb * P : (tb + 1) * P, :], in_=result[:])
+                for cols in (slice(0, HALF), slice(HALF, S)):
+                    nc.scalar.activation(drop[:, cols], root[:, cols], ACT.Square)
+                    nc.vector.tensor_scalar(
+                        result[:, cols], drop[:, cols], neg_idf[:, tb : tb + 1], idf_col[:, tb : tb + 1], ALU.mult, ALU.add
+                    )
+                    nc.sync.dma_start(out=out[rows, cols], in_=result[:, cols])

@@ -38,7 +38,7 @@ def tile_picked_ybm25f_sat_p_kernel(
         idf_col = keep.tile([P, 4], F32, name="idf_col")
         ident = keep.tile([P, P], F32, name="ident", align_bytes=64)
 
-        nc.vector.memset(len_tab[0:96, :], 0.0)
+        nc.vector.memset(len_tab[0 : P - 2, :], 0.0)
 
         def load_scales(queue, f, scales, quadrants):
             for q in quadrants:
@@ -62,8 +62,8 @@ def tile_picked_ybm25f_sat_p_kernel(
         nc.sync.dma_start(offsets[:], offs)
         load_scales(nc.sync, 0, x_scales, range(4))
         load_terms(0)
-        nc.sync.dma_start(out=len_tab[96:112, :], in_=lena[0:16, :])
-        nc.sync.dma_start(out=len_tab[112:128, :], in_=lenb[0:16, :])
+        nc.sync.dma_start(out=len_tab[P - 2 : P - 1, :], in_=lena[0:1, :])
+        nc.sync.dma_start(out=len_tab[P - 1 : P, :], in_=lenb[0:1, :])
         load_words(0, x_words)
         load_terms(1)
         load_scales(nc.sync, 1, e_scales, range(4))
@@ -108,11 +108,10 @@ def tile_picked_ybm25f_sat_p_kernel(
             for f, (slope, base) in enumerate(((0.6 / 2.2, 0.4 / 2.2), (0.75, 0.25))):
                 for s, sign in enumerate((1.0, -1.0)):
                     nc.scalar.activation(
-                        norm[:, f, s, :], turned[:, :, 96 + 16 * f], ACT.Identity, bias=sign * base, scale=sign * slope
+                        norm[:, f, s, :], turned[:, :, P - 2 + f], ACT.Identity, bias=sign * base, scale=sign * slope
                     )
 
         units = [(h, d) for h in range(2) for d in range(2)]
-        sig = keep.tile([P, 2, 4, V], F32, name="sig")
 
         def product(f, dst, b, terms):
             docs = slice(b * P, (b + 1) * P)
@@ -151,10 +150,12 @@ def tile_picked_ybm25f_sat_p_kernel(
         nc.scalar.activation(picked_len[:], len_tab[:].indirect(offsets[:]), ACT.Copy)
         quantize_terms(0)
         gather(words[0], word_tab[0], 0, HALF)
+        cast_terms(1, nc.scalar.copy, slice(0, P))
+        cast_terms(1, nc.vector.tensor_copy, slice(P, HALF))
+        sig = keep.tile([P, 2, 4, V], F32, name="sig", tag="raw1", align_bytes=64)
         title_unit(0)
         gather(words[0], word_tab[0], HALF, HALF)
         title_unit(1)
-        cast_terms(1, nc.vector.tensor_copy, slice(0, HALF))
         quantize_terms(1)
         title_unit(2)
         title_unit(3)
@@ -206,20 +207,26 @@ def tile_picked_ybm25f_sat_p_kernel(
                             is_transpose=True,
                         )
 
-        for tb in range(4):
-            root = keep.tile([P, S], F32, name="root%d" % tb)
-            drop = keep.tile([P, S], F32, name="drop%d" % tb)
-            result = keep.tile([P, S], F32, name="result%d" % tb)
-            rows = slice(tb * P, (tb + 1) * P)
-            nc.scalar.activation(root[:], total[tb][:], ACT.Abs_reciprocal_sqrt, bias=1.2)
-            if tb < 3:
-                nc.vector.scalar_tensor_tensor(drop[:], root[:], neg_idf[:, tb : tb + 1], root[:], ALU.mult, ALU.mult)
-                nc.vector.tensor_scalar(result[:], drop[:], idf_col[:, tb : tb + 1], None, ALU.add)
-                nc.sync.dma_start(out=out[rows, :], in_=result[:])
-            else:
-                for cols in (slice(0, HALF), slice(HALF, S)):
-                    nc.scalar.activation(drop[:, cols], root[:, cols], ACT.Square)
-                    nc.vector.tensor_scalar(
-                        result[:, cols], drop[:, cols], neg_idf[:, tb : tb + 1], idf_col[:, tb : tb + 1], ALU.mult, ALU.add
-                    )
-                    nc.sync.dma_start(out=out[rows, cols], in_=result[:, cols])
+        root = [keep.tile([P, S], F32, name="root%d" % tb) for tb in range(4)]
+        drop = [keep.tile([P, S], F32, name="drop%d" % tb) for tb in range(4)]
+        result = [keep.tile([P, S], F32, name="result%d" % tb) for tb in range(4)]
+
+        def finish(tb):
+            nc.vector.tensor_scalar(result[tb][:], drop[tb][:], idf_col[:, tb : tb + 1], None, ALU.add)
+            nc.sync.dma_start(out=out[tb * P : (tb + 1) * P, :], in_=result[tb][:])
+
+        for tb in range(3):
+            nc.scalar.activation(root[tb][:], total[tb][:], ACT.Abs_reciprocal_sqrt, bias=1.2)
+            nc.vector.scalar_tensor_tensor(
+                drop[tb][:], root[tb][:], neg_idf[:, tb : tb + 1], root[tb][:], ALU.mult, ALU.mult
+            )
+            if tb > 0:
+                finish(tb - 1)
+        finish(2)
+        nc.scalar.activation(root[3][:], total[3][:], ACT.Abs_reciprocal_sqrt, bias=1.2)
+        for cols in (slice(0, HALF), slice(HALF, S)):
+            nc.scalar.activation(drop[3][:, cols], root[3][:, cols], ACT.Square)
+            nc.vector.tensor_scalar(
+                result[3][:, cols], drop[3][:, cols], neg_idf[:, 3:4], idf_col[:, 3:4], ALU.mult, ALU.add
+            )
+            nc.sync.dma_start(out=out[3 * P : 4 * P, cols], in_=result[3][:, cols])

@@ -18,8 +18,24 @@ ALU = mybir.AluOpType
 ACT = mybir.ActivationFunctionType
 
 P = 128
+PACK = 4
+QUADRANT = 32
+BLOCKS = 4
 HALF = 256
+PER_COLUMN = 16
+TITLE, BODY = 0, 1
+LENGTH_ROW = (P - 2, P - 1)
+LENGTH_NORM = ((0.6 / 2.2, 0.4 / 2.2), (0.75, 0.25))
+SATURATION = 1.2
 LOG_FLOOR = 2.0 ** -50
+
+
+def half(h):
+    return slice(h * HALF, (h + 1) * HALF)
+
+
+def block(b):
+    return slice(b * P, (b + 1) * P)
 
 
 def tile_picked_ybm25f_sat_p_kernel(
@@ -30,203 +46,202 @@ def tile_picked_ybm25f_sat_p_kernel(
         keep = ctx.enter_context(tc.tile_pool(name="keep", bufs=1))
         psum = ctx.enter_context(tc.psum_pool(name="psum", bufs=1))
 
-        offsets = keep.tile([P, S // 16], U16, name="offsets")
-        word_tab = [keep.tile([P, T], U32, name="word_tab%d" % f, tag="tab%d" % f, align_bytes=64) for f in range(2)]
-        scale_tab = [keep.tile([P, T], U8, name="scale_tab%d" % f, tag="stab%d" % f, align_bytes=64) for f in range(2)]
-        len_tab = keep.tile([P, T], F32, name="len_tab", align_bytes=64)
-        h_raw = [keep.tile([P, 4, HALF], F32, name="h_raw%d" % h, tag="raw%d" % h, align_bytes=64) for h in range(2)]
-        idf_col = keep.tile([P, 4], F32, name="idf_col")
-        ident = keep.tile([P, P], F32, name="ident", align_bytes=64)
+        def held(shape, dtype, name, tag=None):
+            return keep.tile(shape, dtype, name=name, tag=tag or name, align_bytes=64)
 
-        nc.vector.memset(len_tab[0 : P - 2, :], 0.0)
+        def bank(shape, name, number):
+            return psum.tile(shape, F32, name=name, tag="bank%d" % number)
 
-        def load_scales(queue, f, scales, quadrants):
-            for q in quadrants:
-                queue.dma_start(
-                    out=scale_tab[f][32 * q : 32 * q + 32, :].bitcast(I32),
-                    in_=scales[0, 4 * q : 4 * q + 4, :].bitcast(I32).partition_broadcast(8),
+        offsets = keep.tile([P, S // PER_COLUMN], U16, name="offsets")
+        word_table = [held([P, T], U32, "word_table%d" % f) for f in (TITLE, BODY)]
+        scale_table = [held([P, T], U8, "scale_table%d" % f) for f in (TITLE, BODY)]
+        length_table = held([P, T], F32, "length_table")
+        terms_raw = [held([P, PACK, HALF], F32, "terms_raw%d" % h) for h in range(2)]
+        idf_col = keep.tile([P, BLOCKS], F32, name="idf_col")
+        ident = held([P, P], F32, "ident")
+
+        nc.vector.memset(length_table[0 : LENGTH_ROW[TITLE], :], 0.0)
+
+        def load_scales(f, scale_bytes):
+            for q in range(P // QUADRANT):
+                nc.sync.dma_start(
+                    out=scale_table[f][QUADRANT * q : QUADRANT * (q + 1), :].bitcast(I32),
+                    in_=scale_bytes[0, 4 * q : 4 * q + 4, :].bitcast(I32).partition_broadcast(QUADRANT // 4),
                 )
 
-        def load_words(f, words):
+        def load_words(f, word_bytes):
             nc.sync.dma_start(
-                out=word_tab[f][:].bitcast(I32),
-                in_=words[0].rearrange("p n r -> p (n r)").bitcast(I32),
+                out=word_table[f][:].bitcast(I32),
+                in_=word_bytes[0].rearrange("p n r -> p (n r)").bitcast(I32),
             )
 
         def load_terms(h):
-            nc.sync.dma_start(
-                out=h_raw[h][:],
-                in_=hT[:, h * HALF : (h + 1) * HALF].rearrange("(p r) t -> p r t", r=4),
-            )
+            nc.sync.dma_start(out=terms_raw[h][:], in_=hT[:, half(h)].rearrange("(p r) t -> p r t", r=PACK))
 
         nc.sync.dma_start(offsets[:], offs)
-        load_scales(nc.sync, 0, x_scales, range(4))
+        load_scales(TITLE, x_scales)
         load_terms(0)
-        nc.sync.dma_start(out=len_tab[P - 2 : P - 1, :], in_=lena[0:1, :])
-        nc.sync.dma_start(out=len_tab[P - 1 : P, :], in_=lenb[0:1, :])
-        load_words(0, x_words)
+        for f, lengths in ((TITLE, lena), (BODY, lenb)):
+            nc.sync.dma_start(out=length_table[LENGTH_ROW[f] : LENGTH_ROW[f] + 1, :], in_=lengths[0:1, :])
+        load_words(TITLE, x_words)
         load_terms(1)
-        load_scales(nc.sync, 1, e_scales, range(4))
-        load_words(1, e_words)
-        with nc.allow_non_contiguous_dma(reason="one value a partition"):
+        load_scales(BODY, e_scales)
+        load_words(BODY, e_words)
+        with nc.allow_non_contiguous_dma(reason="idf lies one value a partition: term 128 b + p at [p, b]"):
             nc.sync.dma_start(out=idf_col[:], in_=idf.rearrange("(b p) o -> p (b o)", p=P))
         make_identity(nc, ident[:])
-
-        h_codes = keep.tile([P, V], U32, name="h_codes", align_bytes=64)
-        h_scales = keep.tile([P, V], U8, name="h_scales", align_bytes=64)
-        h_bf = [keep.tile([P, HALF, 4], BF16, name="h_bf%d" % h, align_bytes=64) for h in range(2)]
-        words = [keep.tile([P, S], U32, name="words%d" % f, align_bytes=64) for f in range(2)]
-        scales = [keep.tile([P, S], U8, name="scales%d" % f, align_bytes=64) for f in range(2)]
-
-        def cast_terms(h, copy, cols):
-            copy(
-                out=h_bf[h][:, cols, :].rearrange("p (c i) r -> p c r i", i=4),
-                in_=h_raw[h][:, :, cols].rearrange("p r (c i) -> p c r i", i=4),
-            )
-
-        def quantize_terms(h):
-            nc.vector.quantize_mx(
-                out=h_codes[:, h * HALF : (h + 1) * HALF].bitcast(FP8X4),
-                scales=h_scales[:, h * HALF : (h + 1) * HALF],
-                in_=h_bf[h][:].rearrange("p t r -> p (t r)"),
-            )
-
-        def gather(dst, table, first, count):
-            picked = offsets[:, first // 16 : (first + count) // 16]
-            nc.vector.tensor_copy(dst[:, first : first + count], table[:].indirect(picked))
-
-        factor = keep.tile([P, 2, 2, 4], F32, name="factor", tag="stab1", align_bytes=64)
-        norm = keep.tile([P, 2, 2, 4], F32, name="norm")
 
         warm = keep.tile([P, 2], F32, name="warm")
         nc.vector.memset(warm[:, 0:1], 0.0)
         nc.scalar.activation(warm[:, 1:2], warm[:, 0:1], ACT.Sigmoid)
-        def length_factors():
-            turned = psum.tile([P, 4, P], F32, name="turned", tag="bank7")
-            for b in range(4):
-                nc.tensor.transpose(turned[:, b, :], picked_len[:, b * P : (b + 1) * P], ident[:])
-            for f, (slope, base) in enumerate(((0.6 / 2.2, 0.4 / 2.2), (0.75, 0.25))):
-                for s, sign in enumerate((1.0, -1.0)):
-                    nc.scalar.activation(
-                        norm[:, f, s, :], turned[:, :, P - 2 + f], ACT.Identity, bias=sign * base, scale=sign * slope
-                    )
 
-        units = [(h, d) for h in range(2) for d in range(2)]
+        term_codes = held([P, V], U32, "term_codes")
+        term_scales = held([P, V], U8, "term_scales")
+        terms_bf16 = [held([P, HALF, PACK], BF16, "terms_bf16_%d" % h) for h in range(2)]
+        words = [held([P, S], U32, "words%d" % f) for f in (TITLE, BODY)]
+        scales = [held([P, S], U8, "scales%d" % f) for f in (TITLE, BODY)]
+
+        def round_terms(h, copy, cols):
+            copy(
+                out=terms_bf16[h][:, cols, :].rearrange("p (c i) r -> p c r i", i=4),
+                in_=terms_raw[h][:, :, cols].rearrange("p r (c i) -> p c r i", i=4),
+            )
+
+        def quantize_terms(h):
+            nc.vector.quantize_mx(
+                out=term_codes[:, half(h)].bitcast(FP8X4),
+                scales=term_scales[:, half(h)],
+                in_=terms_bf16[h][:].rearrange("p t r -> p (t r)"),
+            )
+
+        def gather(dst, table, docs):
+            picked = offsets[:, docs.start // PER_COLUMN : docs.stop // PER_COLUMN]
+            nc.vector.tensor_copy(dst[:, docs], table[:].indirect(picked))
+
+        sigmoid = keep.tile([P, 2, BLOCKS, V], F32, name="sigmoid")
+        quarters = [(h, d) for h in range(2) for d in range(2)]
+        title_score, body_score = [], []
 
         def product(f, dst, b, terms):
-            docs = slice(b * P, (b + 1) * P)
             nc.tensor.matmul_mx(
                 out=dst,
-                lhsT=words[f][:, docs].bitcast(FP8X4),
-                lhsT_scale=scales[f][:, docs],
-                rhs=h_codes[:, terms].bitcast(FP8X4),
-                rhs_scale=h_scales[:, terms],
+                lhsT=words[f][:, block(b)].bitcast(FP8X4),
+                lhsT_scale=scales[f][:, block(b)],
+                rhs=term_codes[:, terms].bitcast(FP8X4),
+                rhs_scale=term_scales[:, terms],
                 start=True,
                 stop=True,
             )
 
-        title_score, body_score = [], []
-
-        def title_unit(u):
-            h, d = units[u]
-            terms = slice(h * HALF, (h + 1) * HALF)
-            bank = psum.tile([P, 2, HALF], F32, name="title_score%d" % u, tag="bank%d" % u)
+        def title_quarter(u):
+            h, d = quarters[u]
+            score = bank([P, 2, HALF], "title_score%d" % u, u)
             for i in range(2):
-                product(0, bank[:, i, :], 2 * d + i, terms)
-            title_score.append(bank)
-            nc.scalar.activation(sig[:, 0, 2 * d : 2 * d + 2, terms], bank[:], ACT.Sigmoid, scale=-1.0)
+                product(TITLE, score[:, i, :], 2 * d + i, half(h))
+            title_score.append(score)
+            nc.scalar.activation(sigmoid[:, TITLE, 2 * d : 2 * d + 2, half(h)], score[:], ACT.Sigmoid, scale=-1.0)
 
-        def body_unit(b):
-            bank = psum.tile([P, V], F32, name="body_score%d" % b, tag="bank%d" % (4 + b))
-            product(1, bank[:], b, slice(0, V))
-            body_score.append(bank)
-            nc.scalar.activation(sig[:, 1, b, :], bank[:], ACT.Sigmoid, scale=-1.0)
+        def body_block(b):
+            score = bank([P, V], "body_score%d" % b, BLOCKS + b)
+            product(BODY, score[:], b, slice(0, V))
+            body_score.append(score)
+            nc.scalar.activation(sigmoid[:, BODY, b, :], score[:], ACT.Sigmoid, scale=-1.0)
 
-        gather(scales[0], scale_tab[0], 0, HALF)
-        gather(scales[0], scale_tab[0], HALF, HALF)
-        cast_terms(0, nc.scalar.copy, slice(0, P))
-        cast_terms(0, nc.vector.tensor_copy, slice(P, HALF))
-        picked_len = keep.tile([P, S], F32, name="picked_len", tag="raw0", align_bytes=64)
-        nc.scalar.activation(picked_len[:], len_tab[:].indirect(offsets[:]), ACT.Copy)
-        quantize_terms(0)
-        gather(words[0], word_tab[0], 0, HALF)
-        cast_terms(1, nc.scalar.copy, slice(0, P))
-        cast_terms(1, nc.vector.tensor_copy, slice(P, HALF))
-        sig = keep.tile([P, 2, 4, V], F32, name="sig", tag="raw1", align_bytes=64)
-        title_unit(0)
-        gather(words[0], word_tab[0], HALF, HALF)
-        title_unit(1)
-        quantize_terms(1)
-        title_unit(2)
-        title_unit(3)
-        length_factors()
         for d in range(2):
-            gather(scales[1], scale_tab[1], d * HALF, HALF)
+            gather(scales[TITLE], scale_table[TITLE], half(d))
+        round_terms(0, nc.scalar.copy, block(0))
+        round_terms(0, nc.vector.tensor_copy, block(1))
+        picked_length = held([P, S], F32, "picked_length", tag="terms_raw0")
+        nc.scalar.activation(picked_length[:], length_table[:].indirect(offsets[:]), ACT.Copy)
+        quantize_terms(0)
+        for d in range(2):
+            gather(words[TITLE], word_table[TITLE], half(d))
+            title_quarter(d)
+        round_terms(1, nc.vector.tensor_copy, slice(0, HALF))
+        quantize_terms(1)
+        for d in range(2):
+            title_quarter(2 + d)
+
+        norm = keep.tile([P, 2, 2, BLOCKS], F32, name="norm")
+        turned_length = bank([P, BLOCKS, P], "turned_length", 2 * BLOCKS - 1)
+        for b in range(BLOCKS):
+            nc.tensor.transpose(turned_length[:, b, :], picked_length[:, block(b)], ident[:])
+        for f in (TITLE, BODY):
+            slope, base = LENGTH_NORM[f]
+            for s, sign in enumerate((1.0, -1.0)):
+                nc.scalar.activation(
+                    norm[:, f, s, :], turned_length[:, :, LENGTH_ROW[f]], ACT.Identity, bias=sign * base, scale=sign * slope
+                )
+
+        for d in range(2):
+            gather(scales[BODY], scale_table[BODY], half(d))
             for b in (2 * d, 2 * d + 1):
-                gather(words[1], word_tab[1], b * P, P)
-                body_unit(b)
-        nc.vector.reciprocal(factor[:].rearrange("p f s b -> p (f s b)"), norm[:].rearrange("p f s b -> p (f s b)"))
+                gather(words[BODY], word_table[BODY], block(b))
+                body_block(b)
 
-        neg_idf = keep.tile([P, 4], F32, name="neg_idf")
-        nc.gpsimd.tensor_scalar(neg_idf[:], idf_col[:], -1.2, 0.0, ALU.mult, ALU.add)
+        weight = held([P, 2, 2, BLOCKS], F32, "weight", tag="scale_table%d" % BODY)
+        nc.vector.reciprocal(weight[:].rearrange("p f s b -> p (f s b)"), norm[:].rearrange("p f s b -> p (f s b)"))
 
-        lin = keep.tile([P, 2, 4, V], F32, name="lin", tag="tab1", align_bytes=64)
-        for u, (h, d) in enumerate(units):
+        idf_drop = keep.tile([P, BLOCKS], F32, name="idf_drop")
+        nc.gpsimd.tensor_scalar(idf_drop[:], idf_col[:], -SATURATION, 0.0, ALU.mult, ALU.add)
+
+        linear = held([P, 2, BLOCKS, V], F32, "linear", tag="word_table%d" % BODY)
+        for u, (h, d) in enumerate(quarters):
             for i in range(2):
                 b = 2 * d + i
                 nc.vector.tensor_scalar(
-                    lin[:, 0, b, h * HALF : (h + 1) * HALF], title_score[u][:, i, :], factor[:, 0, 0, b : b + 1], None, ALU.mult
+                    linear[:, TITLE, b, half(h)], title_score[u][:, i, :], weight[:, TITLE, 0, b : b + 1], None, ALU.mult
                 )
-        for b in range(4):
-            nc.vector.tensor_scalar(lin[:, 1, b, :], body_score[b][:], factor[:, 1, 0, b : b + 1], None, ALU.mult)
+        for b in range(BLOCKS):
+            nc.vector.tensor_scalar(linear[:, BODY, b, :], body_score[b][:], weight[:, BODY, 0, b : b + 1], None, ALU.mult)
 
-        total = [psum.tile([P, S], F32, name="total%d" % tb, tag="bank%d" % tb) for tb in range(4)]
-        for u in range(4):
-            h, d = units[u]
-            terms = slice(h * HALF, (h + 1) * HALF)
+        tf = [bank([P, S], "tf%d" % tb, tb) for tb in range(BLOCKS)]
+        for u, (h, d) in enumerate(quarters):
             logs = keep.tile([P, 2, 2, HALF], F32, name="logs%d" % u)
-            nc.scalar.activation(logs[:], sig[:, :, 2 * d : 2 * d + 2, terms], ACT.Ln, bias=LOG_FLOOR)
-            part = keep.tile([P, 2, 2, HALF], F32, name="part%d" % u, align_bytes=64)
+            nc.scalar.activation(logs[:], sigmoid[:, :, 2 * d : 2 * d + 2, half(h)], ACT.Ln, bias=LOG_FLOOR)
+            count = held([P, 2, 2, HALF], F32, "count%d" % u)
             for i in range(2):
                 b = 2 * d + i
-                for f in range(2):
+                for f in (TITLE, BODY):
                     nc.vector.scalar_tensor_tensor(
-                        part[:, f, i, :], logs[:, f, i, :], factor[:, f, 1, b : b + 1],
-                        lin[:, f, b, terms], ALU.mult, ALU.max,
+                        count[:, f, i, :], logs[:, f, i, :], weight[:, f, 1, b : b + 1], linear[:, f, b, half(h)],
+                        ALU.mult, ALU.max,
                     )
             for i in range(2):
-                b = 2 * d + i
                 for e in range(2):
-                    for f in range(2):
+                    for f in (TITLE, BODY):
                         nc.tensor.matmul(
-                            total[2 * h + e][:, b * P : (b + 1) * P],
-                            part[:, f, i, e * P : (e + 1) * P],
+                            tf[2 * h + e][:, block(2 * d + i)],
+                            count[:, f, i, block(e)],
                             ident[:],
-                            start=(f == 0),
-                            stop=(f == 1),
+                            start=(f == TITLE),
+                            stop=(f == BODY),
                             is_transpose=True,
                         )
 
-        root = [keep.tile([P, S], F32, name="root%d" % tb) for tb in range(4)]
-        drop = [keep.tile([P, S], F32, name="drop%d" % tb) for tb in range(4)]
-        result = [keep.tile([P, S], F32, name="result%d" % tb) for tb in range(4)]
+        root = [keep.tile([P, S], F32, name="root%d" % tb) for tb in range(BLOCKS)]
+        last = BLOCKS - 1
+        drop = [keep.tile([P, S], F32, name="drop%d" % tb) for tb in range(last)]
+        square = keep.tile([P, S], F32, name="square")
+        result = [keep.tile([P, S], F32, name="result%d" % tb) for tb in range(BLOCKS)]
 
         def finish(tb):
             nc.vector.tensor_scalar(result[tb][:], drop[tb][:], idf_col[:, tb : tb + 1], None, ALU.add)
-            nc.sync.dma_start(out=out[tb * P : (tb + 1) * P, :], in_=result[tb][:])
+            nc.sync.dma_start(out=out[block(tb), :], in_=result[tb][:])
 
-        for tb in range(3):
-            nc.scalar.activation(root[tb][:], total[tb][:], ACT.Abs_reciprocal_sqrt, bias=1.2)
+        for tb in range(last):
+            nc.scalar.activation(root[tb][:], tf[tb][:], ACT.Abs_reciprocal_sqrt, bias=SATURATION)
             nc.vector.scalar_tensor_tensor(
-                drop[tb][:], root[tb][:], neg_idf[:, tb : tb + 1], root[tb][:], ALU.mult, ALU.mult
+                drop[tb][:], root[tb][:], idf_drop[:, tb : tb + 1], root[tb][:], ALU.mult, ALU.mult
             )
             if tb > 0:
                 finish(tb - 1)
-        finish(2)
-        nc.scalar.activation(root[3][:], total[3][:], ACT.Abs_reciprocal_sqrt, bias=1.2)
-        for cols in (slice(0, HALF), slice(HALF, S)):
-            nc.scalar.activation(drop[3][:, cols], root[3][:, cols], ACT.Square)
+        finish(last - 1)
+        nc.scalar.activation(root[last][:], tf[last][:], ACT.Abs_reciprocal_sqrt, bias=SATURATION)
+        for d in range(2):
+            nc.scalar.activation(square[:, half(d)], root[last][:, half(d)], ACT.Square)
             nc.vector.tensor_scalar(
-                result[3][:, cols], drop[3][:, cols], neg_idf[:, 3:4], idf_col[:, 3:4], ALU.mult, ALU.add
+                result[last][:, half(d)], square[:, half(d)], idf_drop[:, last : last + 1], idf_col[:, last : last + 1],
+                ALU.mult, ALU.add,
             )
-            nc.sync.dma_start(out=out[3 * P : 4 * P, cols], in_=result[3][:, cols])
+            nc.sync.dma_start(out=out[block(last), half(d)], in_=result[last][:, half(d)])

from contextlib import ExitStack

import concourse.mybir as mybir
from concourse.masks import make_identity

K, T, S, V = 512, 1024, 512, 512
FLOPS = 2 * 2 * K * S * V
BYTES = 2 * (K * T + 16 * T) + 4 * K * V + 2 * 4 * T + 4 * V + 2 * 128 * (S // 16) + 4 * V * S

F32 = mybir.dt.float32
BF16 = mybir.dt.bfloat16
I32 = mybir.dt.int32
U32 = mybir.dt.uint32
U16 = mybir.dt.uint16
U8 = mybir.dt.uint8
FP8X4 = mybir.dt.float8_e4m3fn_x4
ALU = mybir.AluOpType
ACT = mybir.ActivationFunctionType

P = 128
PACK = 4
QUADRANT = 32
BLOCKS = 4
HALF = 256
PER_COLUMN = 16
TITLE, BODY = 0, 1
LENGTH_ROW = (P - 2, P - 1)
LENGTH_NORM = ((0.6 / 2.2, 0.4 / 2.2), (0.75, 0.25))
SATURATION = 1.2
LOG_FLOOR = 2.0 ** -50


def half(h):
    return slice(h * HALF, (h + 1) * HALF)


def block(b):
    return slice(b * P, (b + 1) * P)


def tile_picked_ybm25f_sat_p_kernel(
    tc, x_words, x_scales, hT, e_words, e_scales, lena, lenb, idf, offs, out
):
    nc = tc.nc
    with ExitStack() as ctx:
        keep = ctx.enter_context(tc.tile_pool(name="keep", bufs=1))
        psum = ctx.enter_context(tc.psum_pool(name="psum", bufs=1))

        def held(shape, dtype, name, tag=None):
            return keep.tile(shape, dtype, name=name, tag=tag or name, align_bytes=64)

        def bank(shape, name, number):
            return psum.tile(shape, F32, name=name, tag="bank%d" % number)

        offsets = keep.tile([P, S // PER_COLUMN], U16, name="offsets")
        word_table = [held([P, T], U32, "word_table%d" % f) for f in (TITLE, BODY)]
        scale_table = [held([P, T], U8, "scale_table%d" % f) for f in (TITLE, BODY)]
        length_table = held([P, T], F32, "length_table")
        terms_raw = [held([P, PACK, HALF], F32, "terms_raw%d" % h) for h in range(2)]
        idf_col = keep.tile([P, BLOCKS], F32, name="idf_col")
        ident = held([P, P], F32, "ident")

        nc.vector.memset(length_table[0 : LENGTH_ROW[TITLE], :], 0.0)

        def load_scales(f, scale_bytes):
            for q in range(P // QUADRANT):
                nc.sync.dma_start(
                    out=scale_table[f][QUADRANT * q : QUADRANT * (q + 1), :].bitcast(I32),
                    in_=scale_bytes[0, 4 * q : 4 * q + 4, :].bitcast(I32).partition_broadcast(QUADRANT // 4),
                )

        def load_words(f, word_bytes):
            nc.sync.dma_start(
                out=word_table[f][:].bitcast(I32),
                in_=word_bytes[0].rearrange("p n r -> p (n r)").bitcast(I32),
            )

        def load_terms(h):
            nc.sync.dma_start(out=terms_raw[h][:], in_=hT[:, half(h)].rearrange("(p r) t -> p r t", r=PACK))

        nc.sync.dma_start(offsets[:], offs)
        load_scales(TITLE, x_scales)
        load_terms(0)
        for f, lengths in ((TITLE, lena), (BODY, lenb)):
            nc.sync.dma_start(out=length_table[LENGTH_ROW[f] : LENGTH_ROW[f] + 1, :], in_=lengths[0:1, :])
        load_words(TITLE, x_words)
        load_terms(1)
        load_scales(BODY, e_scales)
        load_words(BODY, e_words)
        with nc.allow_non_contiguous_dma(reason="idf lies one value a partition: term 128 b + p at [p, b]"):
            nc.sync.dma_start(out=idf_col[:], in_=idf.rearrange("(b p) o -> p (b o)", p=P))
        make_identity(nc, ident[:])

        warm = keep.tile([P, 2], F32, name="warm")
        nc.vector.memset(warm[:, 0:1], 0.0)
        nc.scalar.activation(warm[:, 1:2], warm[:, 0:1], ACT.Sigmoid)

        term_codes = held([P, V], U32, "term_codes")
        term_scales = held([P, V], U8, "term_scales")
        terms_bf16 = [held([P, HALF, PACK], BF16, "terms_bf16_%d" % h) for h in range(2)]
        words = [held([P, S], U32, "words%d" % f) for f in (TITLE, BODY)]
        scales = [held([P, S], U8, "scales%d" % f) for f in (TITLE, BODY)]

        def round_terms(h, copy, cols):
            copy(
                out=terms_bf16[h][:, cols, :].rearrange("p (c i) r -> p c r i", i=4),
                in_=terms_raw[h][:, :, cols].rearrange("p r (c i) -> p c r i", i=4),
            )

        def quantize_terms(h):
            nc.vector.quantize_mx(
                out=term_codes[:, half(h)].bitcast(FP8X4),
                scales=term_scales[:, half(h)],
                in_=terms_bf16[h][:].rearrange("p t r -> p (t r)"),
            )

        def gather(dst, table, docs):
            picked = offsets[:, docs.start // PER_COLUMN : docs.stop // PER_COLUMN]
            nc.vector.tensor_copy(dst[:, docs], table[:].indirect(picked))

        sigmoid = keep.tile([P, 2, BLOCKS, V], F32, name="sigmoid")
        quarters = [(h, d) for h in range(2) for d in range(2)]
        title_score, body_score = [], []

        def product(f, dst, b, terms):
            nc.tensor.matmul_mx(
                out=dst,
                lhsT=words[f][:, block(b)].bitcast(FP8X4),
                lhsT_scale=scales[f][:, block(b)],
                rhs=term_codes[:, terms].bitcast(FP8X4),
                rhs_scale=term_scales[:, terms],
                start=True,
                stop=True,
            )

        def title_quarter(u):
            h, d = quarters[u]
            score = bank([P, 2, HALF], "title_score%d" % u, u)
            for i in range(2):
                product(TITLE, score[:, i, :], 2 * d + i, half(h))
            title_score.append(score)
            nc.scalar.activation(sigmoid[:, TITLE, 2 * d : 2 * d + 2, half(h)], score[:], ACT.Sigmoid, scale=-1.0)

        def body_block(b):
            score = bank([P, V], "body_score%d" % b, BLOCKS + b)
            product(BODY, score[:], b, slice(0, V))
            body_score.append(score)
            nc.scalar.activation(sigmoid[:, BODY, b, :], score[:], ACT.Sigmoid, scale=-1.0)

        for d in range(2):
            gather(scales[TITLE], scale_table[TITLE], half(d))
        round_terms(0, nc.scalar.copy, block(0))
        round_terms(0, nc.vector.tensor_copy, block(1))
        picked_length = held([P, S], F32, "picked_length", tag="terms_raw0")
        nc.scalar.activation(picked_length[:], length_table[:].indirect(offsets[:]), ACT.Copy)
        quantize_terms(0)
        for d in range(2):
            gather(words[TITLE], word_table[TITLE], half(d))
            title_quarter(d)
        round_terms(1, nc.vector.tensor_copy, slice(0, HALF))
        quantize_terms(1)
        for d in range(2):
            title_quarter(2 + d)

        norm = keep.tile([P, 2, 2, BLOCKS], F32, name="norm")
        turned_length = bank([P, BLOCKS, P], "turned_length", 2 * BLOCKS - 1)
        for b in range(BLOCKS):
            nc.tensor.transpose(turned_length[:, b, :], picked_length[:, block(b)], ident[:])
        for f in (TITLE, BODY):
            slope, base = LENGTH_NORM[f]
            for s, sign in enumerate((1.0, -1.0)):
                nc.scalar.activation(
                    norm[:, f, s, :], turned_length[:, :, LENGTH_ROW[f]], ACT.Identity, bias=sign * base, scale=sign * slope
                )

        for d in range(2):
            gather(scales[BODY], scale_table[BODY], half(d))
            for b in (2 * d, 2 * d + 1):
                gather(words[BODY], word_table[BODY], block(b))
                body_block(b)

        weight = held([P, 2, 2, BLOCKS], F32, "weight", tag="scale_table%d" % BODY)
        nc.vector.reciprocal(weight[:].rearrange("p f s b -> p (f s b)"), norm[:].rearrange("p f s b -> p (f s b)"))

        idf_drop = keep.tile([P, BLOCKS], F32, name="idf_drop")
        nc.gpsimd.tensor_scalar(idf_drop[:], idf_col[:], -SATURATION, 0.0, ALU.mult, ALU.add)

        linear = held([P, 2, BLOCKS, V], F32, "linear", tag="word_table%d" % BODY)
        for u, (h, d) in enumerate(quarters):
            for i in range(2):
                b = 2 * d + i
                nc.vector.tensor_scalar(
                    linear[:, TITLE, b, half(h)], title_score[u][:, i, :], weight[:, TITLE, 0, b : b + 1], None, ALU.mult
                )
        for b in range(BLOCKS):
            nc.vector.tensor_scalar(linear[:, BODY, b, :], body_score[b][:], weight[:, BODY, 0, b : b + 1], None, ALU.mult)

        tf = [bank([P, S], "tf%d" % tb, tb) for tb in range(BLOCKS)]
        for u, (h, d) in enumerate(quarters):
            logs = keep.tile([P, 2, 2, HALF], F32, name="logs%d" % u)
            nc.scalar.activation(logs[:], sigmoid[:, :, 2 * d : 2 * d + 2, half(h)], ACT.Ln, bias=LOG_FLOOR)
            count = held([P, 2, 2, HALF], F32, "count%d" % u)
            for i in range(2):
                b = 2 * d + i
                for f in (TITLE, BODY):
                    nc.vector.scalar_tensor_tensor(
                        count[:, f, i, :], logs[:, f, i, :], weight[:, f, 1, b : b + 1], linear[:, f, b, half(h)],
                        ALU.mult, ALU.max,
                    )
            for i in range(2):
                for e in range(2):
                    for f in (TITLE, BODY):
                        nc.tensor.matmul(
                            tf[2 * h + e][:, block(2 * d + i)],
                            count[:, f, i, block(e)],
                            ident[:],
                            start=(f == TITLE),
                            stop=(f == BODY),
                            is_transpose=True,
                        )

        root = [keep.tile([P, S], F32, name="root%d" % tb) for tb in range(BLOCKS)]
        last = BLOCKS - 1
        drop = [keep.tile([P, S], F32, name="drop%d" % tb) for tb in range(last)]
        square = keep.tile([P, S], F32, name="square")
        result = [keep.tile([P, S], F32, name="result%d" % tb) for tb in range(BLOCKS)]

        def finish(tb):
            nc.vector.tensor_scalar(result[tb][:], drop[tb][:], idf_col[:, tb : tb + 1], None, ALU.add)
            nc.sync.dma_start(out=out[block(tb), :], in_=result[tb][:])

        for tb in range(last):
            nc.scalar.activation(root[tb][:], tf[tb][:], ACT.Abs_reciprocal_sqrt, bias=SATURATION)
            nc.vector.scalar_tensor_tensor(
                drop[tb][:], root[tb][:], idf_drop[:, tb : tb + 1], root[tb][:], ALU.mult, ALU.mult
            )
            if tb > 0:
                finish(tb - 1)
        finish(last - 1)
        nc.scalar.activation(root[last][:], tf[last][:], ACT.Abs_reciprocal_sqrt, bias=SATURATION)
        for d in range(2):
            nc.scalar.activation(square[:, half(d)], root[last][:, half(d)], ACT.Square)
            nc.vector.tensor_scalar(
                result[last][:, half(d)], square[:, half(d)], idf_drop[:, last : last + 1], idf_col[:, last : last + 1],
                ALU.mult, ALU.add,
            )
            nc.sync.dma_start(out=out[block(last), half(d)], in_=result[last][:, half(d)])
